import numpy as np
import ml_dtypes


def mxq(x, axis, fmt="e4m3"):
    dtype, down = {"e4m3": (ml_dtypes.float8_e4m3fn, 7), "e5m2": (ml_dtypes.float8_e5m2, 14)}[fmt]
    v = np.moveaxis(np.asarray(x, np.float32).astype(ml_dtypes.bfloat16).astype(np.float64), axis, -1)
    blocks = v.reshape(v.shape[:-1] + (-1, 32))
    amax = np.abs(blocks).max(-1, keepdims=True)
    byte = np.maximum(np.where(amax > 0, np.frexp(amax)[1] - 1 + 127, 0) - down, 1)
    scale = np.exp2(byte - 127.0)
    codes = (blocks / scale).astype(np.float32).astype(dtype).astype(np.float64)
    return np.moveaxis((codes * scale).reshape(v.shape), -1, axis)


WIDE = False


def mx_kscale(k):
    if not WIDE:
        return np.ones(k)
    levels = np.array([10, -10, 5, -5, 0])
    if k % 512:
        return np.exp2(np.random.permutation(np.resize(levels, k // 32))).repeat(32)
    a = np.empty((k // 512, 16))
    for p in range(k // 512):
        a[p, :8] = np.random.permutation(np.resize(levels, 8))
        for g in range(8):
            far = levels[np.abs(levels - a[p, g]) >= 10]
            a[p, g + 8] = far[np.random.randint(len(far))]
    return np.exp2(a.ravel()).repeat(32)


def f64(x):
    return np.asarray(x).astype(np.float64)


def striped(idx):
    return np.tile(idx.reshape(-1, 16).T, (8, 1)).astype(np.uint16)


def unstriped(offs):
    return offs[:16].T.reshape(-1).astype(np.int64)


E2M1 = np.array([0.0, 0.5, 1.0, 1.5, 2.0, 3.0, 4.0, 6.0, -0.0, -0.5, -1.0, -1.5, -2.0, -3.0, -4.0, -6.0])


def pack_weight(w, fmt):
    k, n = w.shape
    w = f64(np.asarray(w, np.float32).astype(ml_dtypes.bfloat16)).reshape(k // 32, 32, n)
    amax = np.abs(w).max(1)
    if fmt == "e4m3":
        byte = np.frexp(amax)[1] - 1 + 127 - 7
    else:
        mant, ex = np.frexp(amax / 6.0)
        byte = np.where(mant > 0.5, ex, ex - 1) + 127
    byte = np.clip(np.where(amax > 0, byte, 1), 1, 254)
    scaled = (w * np.exp2(127.0 - byte)[:, None, :]).reshape(k, n).astype(np.float32)
    by_word = np.ascontiguousarray(scaled.reshape(k // 512, 128, 4, n).transpose(0, 1, 3, 2))
    if fmt == "e4m3":
        words = by_word.astype(ml_dtypes.float8_e4m3fn).view(np.uint8)
    else:
        c = by_word.astype(ml_dtypes.float4_e2m1fn).view(np.uint8) & 0xF
        words = (c[..., 0::2] | (c[..., 1::2] << 4)).reshape(k // 512, 128, 2 * n)
    return np.ascontiguousarray(words), np.ascontiguousarray(byte.astype(np.uint8).reshape(k // 512, 16, n))


def unpack_weight(words, scales, fmt):
    g, _, n = scales.shape
    words = np.ascontiguousarray(words).reshape(g, 128, n, -1)
    if fmt == "e4m3":
        vals = words.view(ml_dtypes.float8_e4m3fn).astype(np.float64)
    else:
        nib = np.empty((g, 128, n, 4), np.uint8)
        nib[..., 0::2] = words & 0xF
        nib[..., 1::2] = words >> 4
        vals = E2M1[nib]
    vals = vals * np.repeat(np.exp2(scales.astype(np.float64) - 127.0), 8, axis=1)[..., None]
    return vals.transpose(0, 1, 3, 2).reshape(g * 512, n)


def pack_table(v):
    words, scales = pack_weight(v, "e4m3")
    return np.concatenate([words.reshape(words.shape[0], -1), scales.reshape(scales.shape[0], -1)], axis=1)


def unpack_table(tab):
    g, t = tab.shape[0], tab.shape[1] // 528
    return unpack_weight(tab[:, :512 * t].reshape(g, 128, t, 4), tab[:, 512 * t:].reshape(g, 16, t), "e4m3")


K, L, M, T, S = 1536, 1536, 1024, 2048, 1024


def setup_inputs():
    n = np.random.standard_normal
    s1 = mx_kscale(K)[:, None]
    s2 = mx_kscale(L)[:, None]
    p_w4 = pack_weight(n((K, M)) / np.sqrt(K) / s1, "e2m1")
    return {
        "tab": pack_table(n((K, T)) * s1),
        "w4_words": p_w4[0],
        "w4_scales": p_w4[1],
        "tab2": pack_table(n((L, T)) * s2),
        "u": (n((L, M)) / np.sqrt(L) / s2).astype(np.float32),
        "b": (0.3 * n(1024)).astype(np.float32),
        "offs": striped(np.random.permutation(T)[:S]),
        "offs2": striped(np.random.permutation(T)[:S]),
    }


def reference(tab, w4_words, w4_scales, tab2, u, b, offs, offs2):
    tab_ = unpack_table(tab)[:, unstriped(offs)]
    w4_ = unpack_weight(w4_words, w4_scales, "e2m1")
    tab2_ = unpack_table(tab2)[:, unstriped(offs2)]
    u_ = mxq(f64(u), 0, "e4m3")
    y = w4_.T @ tab_ + u_.T @ tab2_
    return y + f64(b)[:, None]

@@ -1,0 +1,199 @@
+from contextlib import ExitStack
+
+import concourse.mybir as mybir
+from concourse.masks import make_identity
+
+K, L, M, T, S = 1536, 1536, 1024, 2048, 1024
+FLOPS = 2 * M * S * (K + L)
+
+F32 = mybir.dt.float32
+BF16 = mybir.dt.bfloat16
+I32 = mybir.dt.int32
+U32 = mybir.dt.uint32
+U16 = mybir.dt.uint16
+U8 = mybir.dt.uint8
+E4M3 = mybir.dt.float8_e4m3fn_x4
+E2M1 = mybir.dt.float4_e2m1fn_x4
+IDENTITY = mybir.ActivationFunctionType.Identity
+ADD = mybir.AluOpType.add
+
+P = 128
+PASSES = K // 512
+MT = 128
+NT = 512
+MH = 512
+
+
+def tile_list_tab2_bias_kernel(tc, tab, w4_words, w4_scales, tab2, u, b, offs, offs2, out):
+    nc = tc.nc
+    with ExitStack() as ctx:
+        keep = ctx.enter_context(tc.tile_pool(name="keep", bufs=1))
+        raws = ctx.enter_context(tc.tile_pool(name="raws", bufs=6))
+        groups = ctx.enter_context(tc.tile_pool(name="groups", bufs=3))
+        outs = ctx.enter_context(tc.tile_pool(name="outs", bufs=8))
+        psum = ctx.enter_context(tc.psum_pool(name="psum", bufs=1))
+
+        offs_sb = keep.tile([P, S // 16], U16, name="offs_sb")
+        offs2_sb = keep.tile([P, S // 16], U16, name="offs2_sb")
+        words = [keep.tile([P, T], I32, name=f"words{a}") for a in range(PASSES)]
+        words2 = [keep.tile([P, T], I32, name=f"words2_{a}") for a in range(PASSES)]
+        planes = keep.tile([P, PASSES, T], U8, name="planes", align_bytes=64)
+        planes2 = keep.tile([P, T], U8, name="planes2", align_bytes=64)
+        w_codes = keep.tile([P, PASSES, 2 * M], U8, name="w_codes", align_bytes=64)
+        w_planes = keep.tile([P, PASSES, M], U8, name="w_planes", align_bytes=64)
+        bias = keep.tile([P, M // MT], F32, name="bias")
+
+        bias_rows = keep.tile([P, P], F32, name="bias_rows")
+        ident = keep.tile([P, P], F32, name="ident")
+        nc.gpsimd.memset(bias_rows[:], 0.0)
+        make_identity(nc, ident[:])
+        nc.vector.memset(planes[:].bitcast(I32), 0)
+        nc.vector.memset(planes2[:].bitcast(I32), 0)
+        nc.vector.memset(w_planes[:].bitcast(I32), 0)
+
+        def load_words(dst, table, a):
+            nc.sync.dma_start(dst[:], table[a, 0 : 512 * T].rearrange("(p w) -> p w", p=P).bitcast(I32))
+
+        tab_scales = tab[:, 512 * T :].rearrange("a (q t) -> q a t", t=T)
+        tab2_scales = tab2[:, 512 * T :].rearrange("a (q t) -> a q t", t=T)
+        w_scale_rows = w4_scales.rearrange("a q n -> q a n")
+        w_word_rows = w4_words.rearrange("a p c -> p a c")
+        raw = {}
+
+        def load_u(h, a):
+            t = raws.tile([P, 4, MH], F32, name="raw")
+            nc.sync.dma_start(t[:], u[512 * a : 512 * (a + 1), MH * h : MH * (h + 1)].rearrange("(p j) w -> p j w", j=4))
+            raw[h, a] = t
+
+        nc.gpsimd.dma_start(bias_rows[0 : M // MT, :], b.rearrange("(m p) -> m p", p=P))
+        nc.sync.dma_start(offs_sb[:], offs)
+        load_words(words[0], tab, 0)
+        for q in range(4):
+            nc.sync.dma_start(planes[32 * q : 32 * q + 4, :, :].bitcast(I32), tab_scales[4 * q : 4 * q + 4].bitcast(I32))
+        load_words(words[1], tab, 1)
+        nc.sync.dma_start(w_codes[:, :, 0:M].bitcast(I32), w_word_rows[:, :, 0:M].bitcast(I32))
+        load_words(words[2], tab, 2)
+        for q in range(4):
+            nc.sync.dma_start(w_planes[32 * q : 32 * q + 4, :, :].bitcast(I32), w_scale_rows[4 * q : 4 * q + 4].bitcast(I32))
+        nc.sync.dma_start(w_codes[:, :, M : 2 * M].bitcast(I32), w_word_rows[:, :, M : 2 * M].bitcast(I32))
+        for a in range(PASSES):
+            load_u(0, a)
+        nc.sync.dma_start(offs2_sb[:], offs2)
+        for q in range(4):
+            nc.sync.dma_start(planes2[32 * q : 32 * q + 12, :].bitcast(I32), tab2_scales[:, 4 * q : 4 * q + 4, :].bitcast(I32))
+        for a in range(PASSES):
+            load_words(words2[a], tab2, a)
+        for a in range(PASSES):
+            load_u(1, a)
+        bias_bank = psum.tile([P, P], F32, name="bank_7")
+        nc.tensor.transpose(bias_bank[:], bias_rows[:], ident[:])
+        nc.scalar.copy(bias[:], bias_bank[:, 0 : M // MT])
+
+        g_words, g_planes, g_words2, g_planes2 = {}, {}, {}, {}
+
+        def gather(window, index, n, dtype, name):
+            t = keep.tile([P, NT], dtype, name=name, align_bytes=64)
+            nc.vector.tensor_copy(t[:], window.indirect(index[:, n * (NT // 16) : (n + 1) * (NT // 16)]))
+            return t
+
+        def gather_tab(n, a):
+            g_words[n, a] = gather(words[a][:].bitcast(U32), offs_sb, n, U32, f"gw_{n}_{a}")
+            g_planes[n, a] = gather(planes[:, a, :], offs_sb, n, U8, f"gp_{n}_{a}")
+
+        u_codes, u_planes = {}, {}
+
+        def group_u(h, a):
+            t = groups.tile([P, MH, 4], BF16, name="grouped", align_bytes=64)
+            nc.scalar.copy(t[:].rearrange("p (c i) t -> p c t i", i=4), raw[h, a][:].rearrange("p t (c i) -> p c t i", i=4))
+            codes = keep.tile([P, MH], U32, name=f"uc_{h}_{a}", align_bytes=64)
+            scales = keep.tile([P, MH], U8, name=f"us_{h}_{a}", align_bytes=64)
+            nc.vector.quantize_mx(out=codes[:].bitcast(E4M3), scales=scales[:], in_=t[:].rearrange("p c t -> p (c t)"))
+            u_codes[h, a], u_planes[h, a] = codes, scales
+
+        acc = {}
+
+        def gather_tab2_planes(n):
+            g_planes2[n] = gather(planes2[:], offs2_sb, n, U8, f"gp2_{n}")
+
+        def gather_tab2(n, a):
+            g_words2[n, a] = gather(words2[a][:].bitcast(U32), offs2_sb, n, U32, f"gw2_{n}_{a}")
+
+        def open_bank(m, n):
+            acc[m, n] = psum.tile([MT, NT], F32, name=f"bank_{m}")
+
+        def mm_w(m, n, a):
+            col = MT * m
+            nc.tensor.matmul_mx(
+                out=acc[m, n][:],
+                lhsT=w_codes[:, a, 2 * col : 2 * (col + MT)].bitcast(E2M1),
+                lhsT_scale=w_planes[:, a, col : col + MT],
+                rhs=g_words[n, a][:].bitcast(E4M3),
+                rhs_scale=g_planes[n, a][:],
+                start=(a == 0),
+                stop=False,
+            )
+
+        def mm_u(m, n, a):
+            h = m // 4
+            cols = slice(MT * (m % 4), MT * (m % 4 + 1))
+            nc.tensor.matmul_mx(
+                out=acc[m, n][:],
+                lhsT=u_codes[h, a][:, cols].bitcast(E4M3),
+                lhsT_scale=u_planes[h, a][:, cols],
+                rhs=g_words2[n, a][:].bitcast(E4M3),
+                rhs_scale=g_planes2[n][4 * a :, :],
+                start=False,
+                stop=(a == PASSES - 1),
+            )
+
+        def empty(m, n, engine):
+            t = outs.tile([MT, NT], F32, name="result")
+            col = bias[:, m : m + 1]
+            if engine == "s":
+                nc.scalar.activation(t[:], acc[m, n][:], IDENTITY, bias=col)
+            else:
+                nc.vector.tensor_scalar(t[:], acc[m, n][:], col, None, op0=ADD)
+            row = MT * m
+            nc.sync.dma_start(out[row : row + MT, NT * n : NT * (n + 1)], t[:])
+
+        for m in range(8):
+            open_bank(m, 0)
+        for a in range(PASSES):
+            gather_tab(0, a)
+            for m in range(8):
+                mm_w(m, 0, a)
+        for a in range(PASSES):
+            group_u(0, a)
+        gather_tab2_planes(0)
+        for a in range(PASSES):
+            gather_tab2(0, a)
+            for m in range(4):
+                mm_u(m, 0, a)
+        for m in range(4):
+            empty(m, 0, "sv"[m % 2])
+        for m in range(4):
+            open_bank(m, 1)
+        for a in range(PASSES):
+            gather_tab(1, a)
+            for m in range(4):
+                mm_w(m, 1, a)
+        for a in range(PASSES):
+            group_u(1, a)
+        gather_tab2_planes(1)
+        for a in range(PASSES):
+            gather_tab2(1, a)
+        for m in range(4):
+            for a in range(PASSES):
+                mm_u(m, 1, a)
+            empty(m, 1, "sv"[m % 2])
+        for m in range(4, 8):
+            for a in range(PASSES):
+                mm_u(m, 0, a)
+            empty(m, 0, "sv"[m % 2])
+        for m in range(4, 8):
+            open_bank(m, 1)
+            for a in range(PASSES):
+                mm_w(m, 1, a)
+            for a in range(PASSES):
+                mm_u(m, 1, a)
+            empty(m, 1, "sv"[m % 2])

@@ -68,24 +68,25 @@ def tile_list_tab2_bias_kernel(tc, tab, w4_words, w4_scales, tab2, u, b, offs, o
         nc.gpsimd.dma_start(bias_rows[0 : M // MT, :], b.rearrange("(m p) -> m p", p=P))
         nc.sync.dma_start(offs_sb[:], offs)
         load_words(words[0], tab, 0)
+        load_words(words[1], tab, 1)
         for q in range(4):
             nc.sync.dma_start(planes[32 * q : 32 * q + 4, :, :].bitcast(I32), tab_scales[4 * q : 4 * q + 4].bitcast(I32))
-        load_words(words[1], tab, 1)
-        nc.sync.dma_start(w_codes[:, :, 0:M].bitcast(I32), w_word_rows[:, :, 0:M].bitcast(I32))
         load_words(words[2], tab, 2)
+        nc.sync.dma_start(w_codes[:, :, 0:M].bitcast(I32), w_word_rows[:, :, 0:M].bitcast(I32))
+        load_u(0, 0)
         for q in range(4):
             nc.sync.dma_start(w_planes[32 * q : 32 * q + 4, :, :].bitcast(I32), w_scale_rows[4 * q : 4 * q + 4].bitcast(I32))
-        nc.sync.dma_start(w_codes[:, :, M : 2 * M].bitcast(I32), w_word_rows[:, :, M : 2 * M].bitcast(I32))
-        for a in range(PASSES):
-            load_u(0, a)
-        nc.sync.dma_start(offs2_sb[:], offs2)
+        load_u(0, 1)
+        load_u(0, 2)
         for q in range(4):
             nc.sync.dma_start(planes2[32 * q : 32 * q + 12, :].bitcast(I32), tab2_scales[:, 4 * q : 4 * q + 4, :].bitcast(I32))
+        nc.sync.dma_start(offs2_sb[:], offs2)
         for a in range(PASSES):
             load_words(words2[a], tab2, a)
+        nc.sync.dma_start(w_codes[:, :, M : 2 * M].bitcast(I32), w_word_rows[:, :, M : 2 * M].bitcast(I32))
         for a in range(PASSES):
             load_u(1, a)
-        bias_bank = psum.tile([P, P], F32, name="bank_7")
+        bias_bank = psum.tile([P, P], F32, name="bank_1_3")
         nc.tensor.transpose(bias_bank[:], bias_rows[:], ident[:])
         nc.scalar.copy(bias[:], bias_bank[:, 0 : M // MT])
 
@@ -98,6 +99,8 @@ def tile_list_tab2_bias_kernel(tc, tab, w4_words, w4_scales, tab2, u, b, offs, o
 
         def gather_tab(n, a):
             g_words[n, a] = gather(words[a][:].bitcast(U32), offs_sb, n, U32, f"gw_{n}_{a}")
+
+        def gather_tab_planes(n, a):
             g_planes[n, a] = gather(planes[:, a, :], offs_sb, n, U8, f"gp_{n}_{a}")
 
         u_codes, u_planes = {}, {}
@@ -119,7 +122,7 @@ def tile_list_tab2_bias_kernel(tc, tab, w4_words, w4_scales, tab2, u, b, offs, o
             g_words2[n, a] = gather(words2[a][:].bitcast(U32), offs2_sb, n, U32, f"gw2_{n}_{a}")
 
         def open_bank(m, n):
-            acc[m, n] = psum.tile([MT, NT], F32, name=f"bank_{m}")
+            acc[m, n] = psum.tile([MT, NT], F32, name=f"bank_{n}_{m % 4}")
 
         def mm_w(m, n, a):
             col = MT * m
@@ -156,44 +159,40 @@ def tile_list_tab2_bias_kernel(tc, tab, w4_words, w4_scales, tab2, u, b, offs, o
             row = MT * m
             nc.sync.dma_start(out[row : row + MT, NT * n : NT * (n + 1)], t[:])
 
-        for m in range(8):
-            open_bank(m, 0)
-        for a in range(PASSES):
-            gather_tab(0, a)
-            for m in range(8):
-                mm_w(m, 0, a)
-        for a in range(PASSES):
-            group_u(0, a)
+        for n in range(2):
+            for m in range(4):
+                open_bank(m, n)
+        for first, last in ((0, 2), (2, 3)):
+            for a in range(first, last):
+                for n in range(2):
+                    gather_tab(n, a)
+            for a in range(first, last):
+                for n in range(2):
+                    gather_tab_planes(n, a)
+                    for m in range(4):
+                        mm_w(m, n, a)
+        group_u(0, 0)
+        group_u(0, 1)
         gather_tab2_planes(0)
+        gather_tab2_planes(1)
+        group_u(0, 2)
         for a in range(PASSES):
-            gather_tab2(0, a)
+            for n in range(2):
+                gather_tab2(n, a)
+                for m in range(4):
+                    mm_u(m, n, a)
+        for n in range(2):
             for m in range(4):
-                mm_u(m, 0, a)
-        for m in range(4):
-            empty(m, 0, "sv"[m % 2])
-        for m in range(4):
-            open_bank(m, 1)
-        for a in range(PASSES):
-            gather_tab(1, a)
-            for m in range(4):
-                mm_w(m, 1, a)
+                empty(m, n, "v")
         for a in range(PASSES):
             group_u(1, a)
-        gather_tab2_planes(1)
-        for a in range(PASSES):
-            gather_tab2(1, a)
-        for m in range(4):
-            for a in range(PASSES):
-                mm_u(m, 1, a)
-            empty(m, 1, "sv"[m % 2])
-        for m in range(4, 8):
-            for a in range(PASSES):
-                mm_u(m, 0, a)
-            empty(m, 0, "sv"[m % 2])
-        for m in range(4, 8):
-            open_bank(m, 1)
-            for a in range(PASSES):
-                mm_w(m, 1, a)
-            for a in range(PASSES):
-                mm_u(m, 1, a)
-            empty(m, 1, "sv"[m % 2])
+        for n in range(2):
+            for m in range(4, 8):
+                open_bank(m, n)
+                for a in range(PASSES):
+                    mm_w(m, n, a)
+        for n in range(2):
+            for m in range(4, 8):
+                for a in range(PASSES):
+                    mm_u(m, n, a)
+                empty(m, n, "sv"[m % 2])

@@ -1,7 +1,6 @@
 from contextlib import ExitStack
 
 import concourse.mybir as mybir
-from concourse.masks import make_identity
 
 K, L, M, T, S = 1536, 1536, 1024, 2048, 1024
 FLOPS = 2 * M * S * (K + L)
@@ -37,24 +36,25 @@ def tile_list_tab2_bias_kernel(tc, tab, w4_words, w4_scales, tab2, u, b, offs, o
         offs2_sb = keep.tile([P, S // 16], U16, name="offs2_sb")
         words = [keep.tile([P, T], I32, name=f"words{a}") for a in range(PASSES)]
         words2 = [keep.tile([P, T], I32, name=f"words2_{a}") for a in range(PASSES)]
-        planes = keep.tile([P, PASSES, T], U8, name="planes", align_bytes=64)
+        planes = keep.tile([P, T], U8, name="planes", align_bytes=64)
         planes2 = keep.tile([P, T], U8, name="planes2", align_bytes=64)
-        w_codes = keep.tile([P, PASSES, 2 * M], U8, name="w_codes", align_bytes=64)
+        w_codes = [keep.tile([P, PASSES, M], U8, name=f"w_codes{h}", align_bytes=64) for h in range(2)]
         w_planes = keep.tile([P, PASSES, M], U8, name="w_planes", align_bytes=64)
         bias = keep.tile([P, M // MT], F32, name="bias")
 
-        bias_rows = keep.tile([P, P], F32, name="bias_rows")
-        ident = keep.tile([P, P], F32, name="ident")
-        nc.gpsimd.memset(bias_rows[:], 0.0)
-        make_identity(nc, ident[:])
         nc.vector.memset(planes[:].bitcast(I32), 0)
-        nc.vector.memset(planes2[:].bitcast(I32), 0)
+        for t in words[1:] + words2:
+            nc.vector.memset(t[:, 0:1], 0)
+        for t in w_codes:
+            nc.vector.memset(t[:].bitcast(I32)[:, :, 0:1], 0)
         nc.vector.memset(w_planes[:].bitcast(I32), 0)
+        nc.vector.memset(planes2[:].bitcast(I32), 0)
+        nc.vector.memset(bias[:], 0.0)
 
         def load_words(dst, table, a):
             nc.sync.dma_start(dst[:], table[a, 0 : 512 * T].rearrange("(p w) -> p w", p=P).bitcast(I32))
 
-        tab_scales = tab[:, 512 * T :].rearrange("a (q t) -> q a t", t=T)
+        tab_scales = tab[:, 512 * T :].rearrange("a (q t) -> a q t", t=T)
         tab2_scales = tab2[:, 512 * T :].rearrange("a (q t) -> a q t", t=T)
         w_scale_rows = w4_scales.rearrange("a q n -> q a n")
         w_word_rows = w4_words.rearrange("a p c -> p a c")
@@ -62,46 +62,49 @@ def tile_list_tab2_bias_kernel(tc, tab, w4_words, w4_scales, tab2, u, b, offs, o
 
         def load_u(h, a):
             t = raws.tile([P, 4, MH], F32, name="raw")
+            nc.vector.memset(t[:, 0, 0:1], 0.0)
             nc.sync.dma_start(t[:], u[512 * a : 512 * (a + 1), MH * h : MH * (h + 1)].rearrange("(p j) w -> p j w", j=4))
             raw[h, a] = t
 
-        nc.gpsimd.dma_start(bias_rows[0 : M // MT, :], b.rearrange("(m p) -> m p", p=P))
-        nc.sync.dma_start(offs_sb[:], offs)
-        load_words(words[0], tab, 0)
-        load_words(words[1], tab, 1)
-        for q in range(4):
-            nc.sync.dma_start(planes[32 * q : 32 * q + 4, :, :].bitcast(I32), tab_scales[4 * q : 4 * q + 4].bitcast(I32))
-        load_words(words[2], tab, 2)
-        nc.sync.dma_start(w_codes[:, :, 0:M].bitcast(I32), w_word_rows[:, :, 0:M].bitcast(I32))
-        load_u(0, 0)
-        for q in range(4):
-            nc.sync.dma_start(w_planes[32 * q : 32 * q + 4, :, :].bitcast(I32), w_scale_rows[4 * q : 4 * q + 4].bitcast(I32))
-        load_u(0, 1)
-        load_u(0, 2)
-        for q in range(4):
-            nc.sync.dma_start(planes2[32 * q : 32 * q + 12, :].bitcast(I32), tab2_scales[:, 4 * q : 4 * q + 4, :].bitcast(I32))
-        nc.sync.dma_start(offs2_sb[:], offs2)
-        for a in range(PASSES):
-            load_words(words2[a], tab2, a)
-        nc.sync.dma_start(w_codes[:, :, M : 2 * M].bitcast(I32), w_word_rows[:, :, M : 2 * M].bitcast(I32))
-        for a in range(PASSES):
-            load_u(1, a)
-        bias_bank = psum.tile([P, P], F32, name="bank_1_3")
-        nc.tensor.transpose(bias_bank[:], bias_rows[:], ident[:])
-        nc.scalar.copy(bias[:], bias_bank[:, 0 : M // MT])
-
         g_words, g_planes, g_words2, g_planes2 = {}, {}, {}, {}
 
-        def gather(window, index, n, dtype, name):
-            t = keep.tile([P, NT], dtype, name=name, align_bytes=64)
-            nc.vector.tensor_copy(t[:], window.indirect(index[:, n * (NT // 16) : (n + 1) * (NT // 16)]))
+        def gather(window, index, first, count, dtype, name):
+            t = keep.tile([P, count], dtype, name=name, align_bytes=64)
+            nc.vector.tensor_copy(t[:], window.indirect(index[:, first // 16 : (first + count) // 16]))
             return t
 
         def gather_tab(n, a):
-            g_words[n, a] = gather(words[a][:].bitcast(U32), offs_sb, n, U32, f"gw_{n}_{a}")
+            g_words[n, a] = gather(words[a][:].bitcast(U32), offs_sb, NT * n, NT, U32, f"gw_{n}_{a}")
 
-        def gather_tab_planes(n, a):
-            g_planes[n, a] = gather(planes[:, a, :], offs_sb, n, U8, f"gp_{n}_{a}")
+        nc.sync.dma_start(offs_sb[:], offs)
+        nc.sync.dma_start(offs2_sb[:], offs2)
+        load_words(words[0], tab, 0)
+        for q in range(4):
+            nc.scalar.dma_start(planes[32 * q : 32 * q + 12, :].bitcast(I32), tab_scales[:, 4 * q : 4 * q + 4, :].bitcast(I32))
+        load_words(words[1], tab, 1)
+        load_words(words[2], tab, 2)
+        nc.sync.dma_start(w_codes[0][:].bitcast(I32), w_word_rows[:, :, 0:M].bitcast(I32))
+        for q in range(4):
+            nc.scalar.dma_start(w_planes[32 * q : 32 * q + 4, :, :].bitcast(I32), w_scale_rows[4 * q : 4 * q + 4].bitcast(I32))
+        for a in range(PASSES):
+            load_u(0, a)
+        for q in range(4):
+            nc.scalar.dma_start(planes2[32 * q : 32 * q + 12, :].bitcast(I32), tab2_scales[:, 4 * q : 4 * q + 4, :].bitcast(I32))
+        g_planes[0] = gather(planes[:], offs_sb, 0, S, U8, "gp_0")
+        for a in range(1, PASSES):
+            g_planes[a] = keep.tile([P, S], U8, name=f"gp_{a}", align_bytes=64)
+            for q in range(4):
+                nc.scalar.dma_start(
+                    g_planes[a][32 * q : 32 * q + 4, :].bitcast(I32),
+                    g_planes[0][32 * q + 4 * a : 32 * q + 4 * a + 4, :].bitcast(I32),
+                )
+        for a in range(PASSES):
+            load_words(words2[a], tab2, a)
+        nc.sync.dma_start(w_codes[1][:].bitcast(I32), w_word_rows[:, :, M : 2 * M].bitcast(I32))
+        for a in range(PASSES):
+            load_u(1, a)
+        with nc.allow_non_contiguous_dma(reason="one bias value a partition"):
+            nc.gpsimd.dma_start(bias[:], b.rearrange("(m p) -> p m", p=P))
 
         u_codes, u_planes = {}, {}
 
@@ -115,11 +118,8 @@ def tile_list_tab2_bias_kernel(tc, tab, w4_words, w4_scales, tab2, u, b, offs, o
 
         acc = {}
 
-        def gather_tab2_planes(n):
-            g_planes2[n] = gather(planes2[:], offs2_sb, n, U8, f"gp2_{n}")
-
         def gather_tab2(n, a):
-            g_words2[n, a] = gather(words2[a][:].bitcast(U32), offs2_sb, n, U32, f"gw2_{n}_{a}")
+            g_words2[n, a] = gather(words2[a][:].bitcast(U32), offs2_sb, NT * n, NT, U32, f"gw2_{n}_{a}")
 
         def open_bank(m, n):
             acc[m, n] = psum.tile([MT, NT], F32, name=f"bank_{n}_{m % 4}")
@@ -128,10 +128,10 @@ def tile_list_tab2_bias_kernel(tc, tab, w4_words, w4_scales, tab2, u, b, offs, o
             col = MT * m
             nc.tensor.matmul_mx(
                 out=acc[m, n][:],
-                lhsT=w_codes[:, a, 2 * col : 2 * (col + MT)].bitcast(E2M1),
+                lhsT=w_codes[m // 4][:, a, 2 * MT * (m % 4) : 2 * MT * (m % 4 + 1)].bitcast(E2M1),
                 lhsT_scale=w_planes[:, a, col : col + MT],
                 rhs=g_words[n, a][:].bitcast(E4M3),
-                rhs_scale=g_planes[n, a][:],
+                rhs_scale=g_planes[a][:, NT * n : NT * (n + 1)],
                 start=(a == 0),
                 stop=False,
             )
@@ -144,7 +144,7 @@ def tile_list_tab2_bias_kernel(tc, tab, w4_words, w4_scales, tab2, u, b, offs, o
                 lhsT=u_codes[h, a][:, cols].bitcast(E4M3),
                 lhsT_scale=u_planes[h, a][:, cols],
                 rhs=g_words2[n, a][:].bitcast(E4M3),
-                rhs_scale=g_planes2[n][4 * a :, :],
+                rhs_scale=g_planes2[0][4 * a :, NT * n : NT * (n + 1)],
                 start=False,
                 stop=(a == PASSES - 1),
             )
@@ -162,20 +162,14 @@ def tile_list_tab2_bias_kernel(tc, tab, w4_words, w4_scales, tab2, u, b, offs, o
         for n in range(2):
             for m in range(4):
                 open_bank(m, n)
-        for first, last in ((0, 2), (2, 3)):
-            for a in range(first, last):
-                for n in range(2):
-                    gather_tab(n, a)
-            for a in range(first, last):
-                for n in range(2):
-                    gather_tab_planes(n, a)
-                    for m in range(4):
-                        mm_w(m, n, a)
-        group_u(0, 0)
-        group_u(0, 1)
-        gather_tab2_planes(0)
-        gather_tab2_planes(1)
-        group_u(0, 2)
+        for a in range(PASSES):
+            for n in range(2):
+                gather_tab(n, a)
+                for m in range(4):
+                    mm_w(m, n, a)
+        g_planes2[0] = gather(planes2[:], offs2_sb, 0, S, U8, "gp2")
+        for a in range(PASSES):
+            group_u(0, a)
         for a in range(PASSES):
             for n in range(2):
                 gather_tab2(n, a)

@@ -1,6 +1,7 @@
 from contextlib import ExitStack
 
 import concourse.mybir as mybir
+from concourse.masks import make_identity
 
 K, L, M, T, S = 1536, 1536, 1024, 2048, 1024
 FLOPS = 2 * M * S * (K + L)
@@ -49,7 +50,10 @@ def tile_list_tab2_bias_kernel(tc, tab, w4_words, w4_scales, tab2, u, b, offs, o
             nc.vector.memset(t[:].bitcast(I32)[:, :, 0:1], 0)
         nc.vector.memset(w_planes[:].bitcast(I32), 0)
         nc.vector.memset(planes2[:].bitcast(I32), 0)
-        nc.vector.memset(bias[:], 0.0)
+        bias_rows = keep.tile([P, P], F32, name="bias_rows")
+        ident = keep.tile([P, P], F32, name="ident")
+        nc.gpsimd.memset(bias_rows[:], 0.0)
+        make_identity(nc, ident[:])
 
         def load_words(dst, table, a):
             nc.sync.dma_start(dst[:], table[a, 0 : 512 * T].rearrange("(p w) -> p w", p=P).bitcast(I32))
@@ -82,35 +86,31 @@ def tile_list_tab2_bias_kernel(tc, tab, w4_words, w4_scales, tab2, u, b, offs, o
         for q in range(4):
             nc.scalar.dma_start(planes[32 * q : 32 * q + 12, :].bitcast(I32), tab_scales[:, 4 * q : 4 * q + 4, :].bitcast(I32))
         load_words(words[1], tab, 1)
-        load_words(words[2], tab, 2)
         nc.sync.dma_start(w_codes[0][:].bitcast(I32), w_word_rows[:, :, 0:M].bitcast(I32))
         for q in range(4):
             nc.scalar.dma_start(w_planes[32 * q : 32 * q + 4, :, :].bitcast(I32), w_scale_rows[4 * q : 4 * q + 4].bitcast(I32))
-        for a in range(PASSES):
-            load_u(0, a)
+        load_words(words[2], tab, 2)
         for q in range(4):
             nc.scalar.dma_start(planes2[32 * q : 32 * q + 12, :].bitcast(I32), tab2_scales[:, 4 * q : 4 * q + 4, :].bitcast(I32))
+        for a in range(PASSES):
+            load_u(0, a)
         g_planes[0] = gather(planes[:], offs_sb, 0, S, U8, "gp_0")
         for a in range(1, PASSES):
             g_planes[a] = keep.tile([P, S], U8, name=f"gp_{a}", align_bytes=64)
-            for q in range(4):
-                nc.scalar.dma_start(
-                    g_planes[a][32 * q : 32 * q + 4, :].bitcast(I32),
-                    g_planes[0][32 * q + 4 * a : 32 * q + 4 * a + 4, :].bitcast(I32),
-                )
+            nc.scalar.dma_start(g_planes[a][0:112, :].bitcast(I32), g_planes[0][4 * a : 112 + 4 * a, :].bitcast(I32))
         for a in range(PASSES):
             load_words(words2[a], tab2, a)
         nc.sync.dma_start(w_codes[1][:].bitcast(I32), w_word_rows[:, :, M : 2 * M].bitcast(I32))
         for a in range(PASSES):
             load_u(1, a)
-        with nc.allow_non_contiguous_dma(reason="one bias value a partition"):
-            nc.gpsimd.dma_start(bias[:], b.rearrange("(m p) -> p m", p=P))
+        nc.gpsimd.dma_start(bias_rows[0 : M // MT, :], b.rearrange("(m p) -> m p", p=P))
 
         u_codes, u_planes = {}, {}
 
-        def group_u(h, a):
+        def group_u(h, a, engine):
             t = groups.tile([P, MH, 4], BF16, name="grouped", align_bytes=64)
-            nc.scalar.copy(t[:].rearrange("p (c i) t -> p c t i", i=4), raw[h, a][:].rearrange("p t (c i) -> p c t i", i=4))
+            copy = nc.scalar.copy if engine == "s" else nc.vector.tensor_copy
+            copy(t[:].rearrange("p (c i) t -> p c t i", i=4), raw[h, a][:].rearrange("p t (c i) -> p c t i", i=4))
             codes = keep.tile([P, MH], U32, name=f"uc_{h}_{a}", align_bytes=64)
             scales = keep.tile([P, MH], U8, name=f"us_{h}_{a}", align_bytes=64)
             nc.vector.quantize_mx(out=codes[:].bitcast(E4M3), scales=scales[:], in_=t[:].rearrange("p c t -> p (c t)"))
@@ -159,6 +159,9 @@ def tile_list_tab2_bias_kernel(tc, tab, w4_words, w4_scales, tab2, u, b, offs, o
             row = MT * m
             nc.sync.dma_start(out[row : row + MT, NT * n : NT * (n + 1)], t[:])
 
+        bias_bank = psum.tile([P, P], F32, name="bank_1_3")
+        nc.tensor.transpose(bias_bank[:], bias_rows[:], ident[:])
+        nc.vector.tensor_copy(bias[:], bias_bank[:, 0 : M // MT])
         for n in range(2):
             for m in range(4):
                 open_bank(m, n)
@@ -169,7 +172,7 @@ def tile_list_tab2_bias_kernel(tc, tab, w4_words, w4_scales, tab2, u, b, offs, o
                     mm_w(m, n, a)
         g_planes2[0] = gather(planes2[:], offs2_sb, 0, S, U8, "gp2")
         for a in range(PASSES):
-            group_u(0, a)
+            group_u(0, a, "s")
         for a in range(PASSES):
             for n in range(2):
                 gather_tab2(n, a)
@@ -179,7 +182,7 @@ def tile_list_tab2_bias_kernel(tc, tab, w4_words, w4_scales, tab2, u, b, offs, o
             for m in range(4):
                 empty(m, n, "v")
         for a in range(PASSES):
-            group_u(1, a)
+            group_u(1, a, "ssv"[a])
         for n in range(2):
             for m in range(4, 8):
                 open_bank(m, n)

from contextlib import ExitStack

import concourse.mybir as mybir
from concourse.masks import make_identity

K, L, M, T, S = 1536, 1536, 1024, 2048, 1024
FLOPS = 2 * M * S * (K + L)

F32 = mybir.dt.float32
BF16 = mybir.dt.bfloat16
I32 = mybir.dt.int32
U32 = mybir.dt.uint32
U16 = mybir.dt.uint16
U8 = mybir.dt.uint8
E4M3 = mybir.dt.float8_e4m3fn_x4
E2M1 = mybir.dt.float4_e2m1fn_x4
IDENTITY = mybir.ActivationFunctionType.Identity
ADD = mybir.AluOpType.add

P = 128
PASSES = K // 512
MT = 128
NT = 512
MH = 512


def tile_list_tab2_bias_kernel(tc, tab, w4_words, w4_scales, tab2, u, b, offs, offs2, out):
    nc = tc.nc
    with ExitStack() as ctx:
        keep = ctx.enter_context(tc.tile_pool(name="keep", bufs=1))
        raws = ctx.enter_context(tc.tile_pool(name="raws", bufs=6))
        groups = ctx.enter_context(tc.tile_pool(name="groups", bufs=3))
        outs = ctx.enter_context(tc.tile_pool(name="outs", bufs=8))
        psum = ctx.enter_context(tc.psum_pool(name="psum", bufs=1))

        offs_sb = keep.tile([P, S // 16], U16, name="offs_sb")
        offs2_sb = keep.tile([P, S // 16], U16, name="offs2_sb")
        words = [keep.tile([P, T], I32, name=f"words{a}") for a in range(PASSES)]
        words2 = [keep.tile([P, T], I32, name=f"words2_{a}") for a in range(PASSES)]
        planes = keep.tile([P, T], U8, name="planes", align_bytes=64)
        planes2 = keep.tile([P, T], U8, name="planes2", align_bytes=64)
        w_codes = [keep.tile([P, PASSES, M], U8, name=f"w_codes{h}", align_bytes=64) for h in range(2)]
        w_planes = keep.tile([P, PASSES, M], U8, name="w_planes", align_bytes=64)
        bias = keep.tile([P, M // MT], F32, name="bias")

        nc.vector.memset(planes[:].bitcast(I32), 0)
        for t in words[1:] + words2:
            nc.vector.memset(t[:, 0:1], 0)
        for t in w_codes:
            nc.vector.memset(t[:].bitcast(I32)[:, :, 0:1], 0)
        nc.vector.memset(w_planes[:].bitcast(I32), 0)
        nc.vector.memset(planes2[:].bitcast(I32), 0)
        bias_rows = keep.tile([P, P], F32, name="bias_rows")
        ident = keep.tile([P, P], F32, name="ident")
        nc.gpsimd.memset(bias_rows[:], 0.0)
        make_identity(nc, ident[:])

        def load_words(dst, table, a):
            nc.sync.dma_start(dst[:], table[a, 0 : 512 * T].rearrange("(p w) -> p w", p=P).bitcast(I32))

        tab_scales = tab[:, 512 * T :].rearrange("a (q t) -> a q t", t=T)
        tab2_scales = tab2[:, 512 * T :].rearrange("a (q t) -> a q t", t=T)
        w_scale_rows = w4_scales.rearrange("a q n -> q a n")
        w_word_rows = w4_words.rearrange("a p c -> p a c")
        raw = {}

        def load_u(h, a):
            t = raws.tile([P, 4, MH], F32, name="raw")
            nc.vector.memset(t[:, 0, 0:1], 0.0)
            nc.sync.dma_start(t[:], u[512 * a : 512 * (a + 1), MH * h : MH * (h + 1)].rearrange("(p j) w -> p j w", j=4))
            raw[h, a] = t

        g_words, g_planes, g_words2, g_planes2 = {}, {}, {}, {}

        def gather(window, index, first, count, dtype, name):
            t = keep.tile([P, count], dtype, name=name, align_bytes=64)
            nc.vector.tensor_copy(t[:], window.indirect(index[:, first // 16 : (first + count) // 16]))
            return t

        def gather_tab(n, a):
            g_words[n, a] = gather(words[a][:].bitcast(U32), offs_sb, NT * n, NT, U32, f"gw_{n}_{a}")

        nc.sync.dma_start(offs_sb[:], offs)
        nc.sync.dma_start(offs2_sb[:], offs2)
        load_words(words[0], tab, 0)
        for q in range(4):
            nc.scalar.dma_start(planes[32 * q : 32 * q + 12, :].bitcast(I32), tab_scales[:, 4 * q : 4 * q + 4, :].bitcast(I32))
        load_words(words[1], tab, 1)
        nc.sync.dma_start(w_codes[0][:].bitcast(I32), w_word_rows[:, :, 0:M].bitcast(I32))
        for q in range(4):
            nc.scalar.dma_start(w_planes[32 * q : 32 * q + 4, :, :].bitcast(I32), w_scale_rows[4 * q : 4 * q + 4].bitcast(I32))
        load_words(words[2], tab, 2)
        for q in range(4):
            nc.scalar.dma_start(planes2[32 * q : 32 * q + 12, :].bitcast(I32), tab2_scales[:, 4 * q : 4 * q + 4, :].bitcast(I32))
        for a in range(PASSES):
            load_u(0, a)
        g_planes[0] = gather(planes[:], offs_sb, 0, S, U8, "gp_0")
        for a in range(1, PASSES):
            g_planes[a] = keep.tile([P, S], U8, name=f"gp_{a}", align_bytes=64)
            nc.scalar.dma_start(g_planes[a][0:112, :].bitcast(I32), g_planes[0][4 * a : 112 + 4 * a, :].bitcast(I32))
        for a in range(PASSES):
            load_words(words2[a], tab2, a)
        nc.sync.dma_start(w_codes[1][:].bitcast(I32), w_word_rows[:, :, M : 2 * M].bitcast(I32))
        for a in range(PASSES):
            load_u(1, a)
        nc.gpsimd.dma_start(bias_rows[0 : M // MT, :], b.rearrange("(m p) -> m p", p=P))

        u_codes, u_planes = {}, {}

        def group_u(h, a, engine):
            t = groups.tile([P, MH, 4], BF16, name="grouped", align_bytes=64)
            copy = nc.scalar.copy if engine == "s" else nc.vector.tensor_copy
            copy(t[:].rearrange("p (c i) t -> p c t i", i=4), raw[h, a][:].rearrange("p t (c i) -> p c t i", i=4))
            codes = keep.tile([P, MH], U32, name=f"uc_{h}_{a}", align_bytes=64)
            scales = keep.tile([P, MH], U8, name=f"us_{h}_{a}", align_bytes=64)
            nc.vector.quantize_mx(out=codes[:].bitcast(E4M3), scales=scales[:], in_=t[:].rearrange("p c t -> p (c t)"))
            u_codes[h, a], u_planes[h, a] = codes, scales

        acc = {}

        def gather_tab2(n, a):
            g_words2[n, a] = gather(words2[a][:].bitcast(U32), offs2_sb, NT * n, NT, U32, f"gw2_{n}_{a}")

        def open_bank(m, n):
            acc[m, n] = psum.tile([MT, NT], F32, name=f"bank_{n}_{m % 4}")

        def mm_w(m, n, a):
            col = MT * m
            nc.tensor.matmul_mx(
                out=acc[m, n][:],
                lhsT=w_codes[m // 4][:, a, 2 * MT * (m % 4) : 2 * MT * (m % 4 + 1)].bitcast(E2M1),
                lhsT_scale=w_planes[:, a, col : col + MT],
                rhs=g_words[n, a][:].bitcast(E4M3),
                rhs_scale=g_planes[a][:, NT * n : NT * (n + 1)],
                start=(a == 0),
                stop=False,
            )

        def mm_u(m, n, a):
            h = m // 4
            cols = slice(MT * (m % 4), MT * (m % 4 + 1))
            nc.tensor.matmul_mx(
                out=acc[m, n][:],
                lhsT=u_codes[h, a][:, cols].bitcast(E4M3),
                lhsT_scale=u_planes[h, a][:, cols],
                rhs=g_words2[n, a][:].bitcast(E4M3),
                rhs_scale=g_planes2[0][4 * a :, NT * n : NT * (n + 1)],
                start=False,
                stop=(a == PASSES - 1),
            )

        def empty(m, n, engine):
            t = outs.tile([MT, NT], F32, name="result")
            col = bias[:, m : m + 1]
            if engine == "s":
                nc.scalar.activation(t[:], acc[m, n][:], IDENTITY, bias=col)
            else:
                nc.vector.tensor_scalar(t[:], acc[m, n][:], col, None, op0=ADD)
            row = MT * m
            nc.sync.dma_start(out[row : row + MT, NT * n : NT * (n + 1)], t[:])

        bias_bank = psum.tile([P, P], F32, name="bank_1_3")
        nc.tensor.transpose(bias_bank[:], bias_rows[:], ident[:])
        nc.vector.tensor_copy(bias[:], bias_bank[:, 0 : M // MT])
        for n in range(2):
            for m in range(4):
                open_bank(m, n)
        for a in range(PASSES):
            for n in range(2):
                gather_tab(n, a)
                for m in range(4):
                    mm_w(m, n, a)
        g_planes2[0] = gather(planes2[:], offs2_sb, 0, S, U8, "gp2")
        for a in range(PASSES):
            group_u(0, a, "s")
        for a in range(PASSES):
            for n in range(2):
                gather_tab2(n, a)
                for m in range(4):
                    mm_u(m, n, a)
        for n in range(2):
            for m in range(4):
                empty(m, n, "v")
        for a in range(PASSES):
            group_u(1, a, "ssv"[a])
        for n in range(2):
            for m in range(4, 8):
                open_bank(m, n)
                for a in range(PASSES):
                    mm_w(m, n, a)
        for n in range(2):
            for m in range(4, 8):
                for a in range(PASSES):
                    mm_u(m, n, a)
                empty(m, n, "sv"[m % 2])
